import numpy as np
import ml_dtypes


def mxq(x, axis, fmt="e4m3"):
    dtype, down = {"e4m3": (ml_dtypes.float8_e4m3fn, 7), "e5m2": (ml_dtypes.float8_e5m2, 14)}[fmt]
    v = np.moveaxis(np.asarray(x, np.float32).astype(ml_dtypes.bfloat16).astype(np.float64), axis, -1)
    blocks = v.reshape(v.shape[:-1] + (-1, 32))
    amax = np.abs(blocks).max(-1, keepdims=True)
    byte = np.maximum(np.where(amax > 0, np.frexp(amax)[1] - 1 + 127, 0) - down, 1)
    scale = np.exp2(byte - 127.0)
    codes = (blocks / scale).astype(np.float32).astype(dtype).astype(np.float64)
    return np.moveaxis((codes * scale).reshape(v.shape), -1, axis)


WIDE = False


def mx_kscale(k):
    if not WIDE:
        return np.ones(k)
    levels = np.array([10, -10, 5, -5, 0])
    if k % 512:
        return np.exp2(np.random.permutation(np.resize(levels, k // 32))).repeat(32)
    a = np.empty((k // 512, 16))
    for p in range(k // 512):
        a[p, :8] = np.random.permutation(np.resize(levels, 8))
        for g in range(8):
            far = levels[np.abs(levels - a[p, g]) >= 10]
            a[p, g + 8] = far[np.random.randint(len(far))]
    return np.exp2(a.ravel()).repeat(32)


def f64(x):
    return np.asarray(x).astype(np.float64)


def striped8(idx):
    return np.asarray(idx).reshape(8, -1, 16).transpose(0, 2, 1).reshape(128, -1).astype(np.uint16)


def unstriped8(offs):
    return offs.reshape(8, 16, -1).transpose(0, 2, 1).reshape(8, -1).astype(np.int64)


def pick8(x, idx, run):
    r = np.arange(len(x))
    return x[r[:, None], idx[r % (8 * run) // run]]


E2M1 = np.array([0.0, 0.5, 1.0, 1.5, 2.0, 3.0, 4.0, 6.0, -0.0, -0.5, -1.0, -1.5, -2.0, -3.0, -4.0, -6.0])


def pack_weight(w, fmt):
    k, n = w.shape
    w = f64(np.asarray(w, np.float32).astype(ml_dtypes.bfloat16)).reshape(k // 32, 32, n)
    amax = np.abs(w).max(1)
    if fmt == "e4m3":
        byte = np.frexp(amax)[1] - 1 + 127 - 7
    else:
        mant, ex = np.frexp(amax / 6.0)
        byte = np.where(mant > 0.5, ex, ex - 1) + 127
    byte = np.clip(np.where(amax > 0, byte, 1), 1, 254)
    scaled = (w * np.exp2(127.0 - byte)[:, None, :]).reshape(k, n).astype(np.float32)
    by_word = np.ascontiguousarray(scaled.reshape(k // 512, 128, 4, n).transpose(0, 1, 3, 2))
    if fmt == "e4m3":
        words = by_word.astype(ml_dtypes.float8_e4m3fn).view(np.uint8)
    else:
        c = by_word.astype(ml_dtypes.float4_e2m1fn).view(np.uint8) & 0xF
        words = (c[..., 0::2] | (c[..., 1::2] << 4)).reshape(k // 512, 128, 2 * n)
    return np.ascontiguousarray(words), np.ascontiguousarray(byte.astype(np.uint8).reshape(k // 512, 16, n))


def unpack_weight(words, scales, fmt):
    g, _, n = scales.shape
    words = np.ascontiguousarray(words).reshape(g, 128, n, -1)
    if fmt == "e4m3":
        vals = words.view(ml_dtypes.float8_e4m3fn).astype(np.float64)
    else:
        nib = np.empty((g, 128, n, 4), np.uint8)
        nib[..., 0::2] = words & 0xF
        nib[..., 1::2] = words >> 4
        vals = E2M1[nib]
    vals = vals * np.repeat(np.exp2(scales.astype(np.float64) - 127.0), 8, axis=1)[..., None]
    return vals.transpose(0, 1, 3, 2).reshape(g * 512, n)


D, K, T, U, X, S, I, Q = 512, 512, 1024, 1024, 1024, 1024, 512, 128


def setup_inputs():
    n = np.random.standard_normal
    idx = np.stack([np.random.permutation(T)[:I] for _ in range(8)])
    idx2 = np.stack([np.random.permutation(U)[:I] for _ in range(8)])
    idx3 = np.stack([np.random.permutation(X)[:I] for _ in range(8)])
    idx4 = np.stack([np.random.permutation(S)[:I] for _ in range(8)])
    idx5 = np.stack([np.random.permutation(X)[:I] for _ in range(8)])
    fd = mx_kscale(D)
    fk = mx_kscale(K)
    wqp = pack_weight(n((D, K)) * 1.0 / np.sqrt(D) * fd[:, None] * fk, "e4m3")
    keysp = pack_weight(n((K, T)) * 1.0 / np.sqrt(K) / fk[:, None], "e4m3")
    notesp = pack_weight(n((K, U)) * 1.0 / np.sqrt(K) / fk[:, None], "e2m1")
    usersp = pack_weight(n((D, X)) * 1.0 / np.sqrt(D) * fd[:, None], "e4m3")
    shelvesp = pack_weight(n((D, S)) * 1.0 / np.sqrt(D) * fd[:, None], "e2m1")
    return {
        "states": (n((D, Q)) * 0.95 / fd[:, None]).astype(np.float32),
        "wq_words": wqp[0],
        "wq_scales": wqp[1],
        "keys_words": keysp[0],
        "keys_scales": keysp[1],
        "notes_words": notesp[0],
        "notes_scales": notesp[1],
        "users_words": usersp[0],
        "users_scales": usersp[1],
        "shelves_words": shelvesp[0],
        "shelves_scales": shelvesp[1],
        "offs": striped8(idx),
        "offs2": striped8(idx2),
        "offs3": striped8(idx3),
        "offs4": striped8(idx4),
        "offs5": striped8(idx5),
    }


def reference(states, wq_words, wq_scales, keys_words, keys_scales, notes_words, notes_scales, users_words, users_scales, shelves_words, shelves_scales, offs, offs2, offs3, offs4, offs5):
    idx = unstriped8(offs)
    idx2 = unstriped8(offs2)
    idx3 = unstriped8(offs3)
    idx4 = unstriped8(offs4)
    idx5 = unstriped8(offs5)
    wqu = unpack_weight(wq_words, wq_scales, "e4m3")
    keysu = unpack_weight(keys_words, keys_scales, "e4m3")
    notesu = unpack_weight(notes_words, notes_scales, "e2m1")
    usersu = unpack_weight(users_words, users_scales, "e4m3")
    shelvesu = unpack_weight(shelves_words, shelves_scales, "e2m1")
    statesq = mxq(f64(states), 0, "e4m3")
    qv = wqu.T @ statesq
    qvq = mxq(qv, 0, "e4m3")
    a = qvq.T @ keysu
    b = qvq.T @ notesu
    c0 = statesq.T @ usersu
    d0 = statesq.T @ shelvesu
    w = np.maximum(pick8(a, idx, 16), pick8(d0, idx4, 16))
    r = np.minimum(w, pick8(b, idx2, 16))
    v = r - pick8(c0, idx3, 16)
    f1 = np.zeros((Q, X))
    f1[np.arange(Q)[:, None], idx3[np.arange(Q) % 128 // 16]] = v
    cc = c0 + f1
    y = pick8(cc, idx5, 16) + w
    return y

@@ -1,0 +1,217 @@
+from contextlib import ExitStack
+
+import concourse.mybir as mybir
+
+D, K, COLS, SLOTS, Q = 512, 512, 1024, 512, 128
+FLOPS = 2 * D * K * Q + 4 * 2 * K * COLS * Q
+
+F32 = mybir.dt.float32
+BF16 = mybir.dt.bfloat16
+I32 = mybir.dt.int32
+U32 = mybir.dt.uint32
+U16 = mybir.dt.uint16
+U8 = mybir.dt.uint8
+FP8X4 = mybir.dt.float8_e4m3fn_x4
+FP4X4 = mybir.dt.float4_e2m1fn_x4
+ALU = mybir.AluOpType
+COPY = mybir.ActivationFunctionType.Copy
+
+P = 128
+PACK = 4
+BANK = 512
+HALF = SLOTS // 2
+LIST_COLS = HALF // 16
+
+
+def tile_attend_substitutes_madefour_kernel(
+    tc, states, wq_words, wq_scales, keys_words, keys_scales, notes_words, notes_scales,
+    users_words, users_scales, shelves_words, shelves_scales, offs, offs2, offs3, offs4, offs5, out,
+):
+    nc = tc.nc
+    with ExitStack() as ctx:
+        lists = ctx.enter_context(tc.tile_pool(name="lists", bufs=1))
+        keep = ctx.enter_context(tc.tile_pool(name="keep", bufs=1))
+        psum = ctx.enter_context(tc.psum_pool(name="psum", bufs=1))
+
+        def zeroed_scales(engine, name, width):
+            tile = keep.tile([P, width], U8, name=name, align_bytes=64)
+            engine.memset(tile[:].bitcast(I32), 0)
+            return tile
+
+        def load_scales(queue, tile, scales, which=range(4)):
+            rows = scales[0].rearrange("(quad r) n -> r quad n", r=4)
+            for r in which:
+                queue.dma_start(tile[r:P:32, :].bitcast(I32), rows[r].bitcast(I32))
+
+        def load_fp8(queue, name, words):
+            tile = keep.tile([P, words.shape[2]], U32, name=name, align_bytes=64)
+            queue.dma_start(tile[:].bitcast(I32), words[0].rearrange("p n t -> p (n t)").bitcast(I32))
+            return tile
+
+        def load_fp4(queue, name, words):
+            tile = keep.tile([P, words.shape[2]], U8, name=name, align_bytes=64)
+            queue.dma_start(tile[:].bitcast(I32), words[0].bitcast(I32))
+            return tile
+
+        def load_list(name, source):
+            tile = lists.tile([P, SLOTS // 16], U16, name=name)
+            nc.sync.dma_start(tile[:], source)
+            return tile
+
+        keys_sc = zeroed_scales(nc.gpsimd, "keys_sc", COLS)
+        wq_sc = zeroed_scales(nc.vector, "wq_sc", K)
+        shelves_sc = zeroed_scales(nc.vector, "shelves_sc", COLS)
+        users_sc = zeroed_scales(nc.vector, "users_sc", COLS)
+        notes_sc = zeroed_scales(nc.vector, "notes_sc", COLS)
+        f1 = keep.tile([P, COLS], F32, name="f1")
+        states_sb = keep.tile([P, PACK, Q], F32, name="states_sb")
+        nc.vector.memset(f1[:], 0.0)
+        load_scales(nc.scalar, wq_sc, wq_scales)
+        nc.sync.dma_start(states_sb[:], states.rearrange("(p t) q -> p t q", t=PACK))
+        wq_raw = load_fp8(nc.sync, "wq_raw", wq_words)
+        shelves_w = load_fp4(nc.sync, "shelves_w", shelves_words)
+        load_scales(nc.gpsimd, keys_sc, keys_scales, (0, 1))
+        users_w = load_fp8(nc.gpsimd, "users_w", users_words)
+        notes_w = load_fp4(nc.gpsimd, "notes_w", notes_words)
+        keys_w = load_fp8(nc.gpsimd, "keys_w", keys_words)
+        load_scales(nc.gpsimd, keys_sc, keys_scales, (2, 3))
+        load_scales(nc.sync, shelves_sc, shelves_scales)
+        load_scales(nc.sync, users_sc, users_scales)
+        idx4 = load_list("idx4", offs4)
+        load_scales(nc.sync, notes_sc, notes_scales)
+        idx3 = load_list("idx3", offs3)
+        idx2 = load_list("idx2", offs2)
+        idx = load_list("idx", offs)
+        idx5 = load_list("idx5", offs5)
+
+        def quantise(name, grouped):
+            codes = keep.tile([P, Q], U32, name=name + "_codes", align_bytes=64)
+            scales = keep.tile([P, Q], U8, name=name + "_scales", align_bytes=64)
+            nc.vector.quantize_mx(
+                out=codes[:].bitcast(FP8X4), scales=scales[:], in_=grouped[:].rearrange("p q t -> p (q t)")
+            )
+            return codes, scales
+
+        wq_sc_dealt = keep.tile([P, K], U8, name="wq_sc_dealt", align_bytes=64)
+        wq_dealt = keep.tile([P, K], U32, name="wq_dealt", align_bytes=64)
+        states_bf = keep.tile([P, Q, PACK], BF16, name="states_bf", align_bytes=64)
+        nc.vector.tensor_copy(
+            wq_sc_dealt[:].rearrange("p (t m) -> p m t", t=PACK), wq_sc[:].rearrange("p (m t) -> p m t", t=PACK)
+        )
+        nc.vector.tensor_copy(states_bf[:], states_sb[:].rearrange("p t q -> p q t"))
+        nc.vector.tensor_copy(
+            wq_dealt[:].bitcast(I32).rearrange("p (t m) -> p m t", t=PACK),
+            wq_raw[:].bitcast(I32).rearrange("p (m t) -> p m t", t=PACK),
+        )
+        st_codes, st_scales = quantise("st", states_bf)
+
+        qv_bank = psum.tile([P, PACK, Q], F32, name="qv_bank", tag="shared")
+        def make_qv():
+            for t in range(PACK):
+                cols = slice(t * P, (t + 1) * P)
+                nc.tensor.matmul_mx(
+                    out=qv_bank[:, t, :],
+                    lhsT=wq_dealt[:, cols].bitcast(FP8X4), lhsT_scale=wq_sc_dealt[:, cols],
+                    rhs=st_codes[:].bitcast(FP8X4), rhs_scale=st_scales[:],
+                    start=True, stop=True,
+                )
+
+        def product(tag, codes, scales, words, word_scales, fp4, half):
+            bank = psum.tile([P, BANK], F32, name="bank_" + tag, tag=tag)
+            cols = slice(half * BANK, (half + 1) * BANK)
+            if fp4:
+                moving = words[:, 2 * cols.start : 2 * cols.stop].bitcast(FP4X4)
+            else:
+                moving = words[:, cols].bitcast(FP8X4)
+            nc.tensor.matmul_mx(
+                out=bank[:], lhsT=codes[:].bitcast(FP8X4), lhsT_scale=scales[:],
+                rhs=moving, rhs_scale=word_scales[:, cols], start=True, stop=True,
+            )
+            return bank
+
+        a_sb = keep.tile([P, COLS], F32, name="a_sb")
+        b_sb = keep.tile([P, COLS], F32, name="b_sb")
+        c0_sb = keep.tile([P, COLS], F32, name="c0_sb")
+        d0_sb = keep.tile([P, COLS], F32, name="d0_sb")
+        cc = keep.tile([P, COLS], F32, name="cc")
+        a_g = keep.tile([P, SLOTS], F32, name="a_g")
+        w = keep.tile([P, SLOTS], F32, name="w")
+        r = keep.tile([P, SLOTS], F32, name="r")
+        cc_g = keep.tile([P, HALF], F32, name="cc_g")
+        y = keep.tile([P, SLOTS], F32, name="y")
+        qv_bf = keep.tile([P, Q, PACK], BF16, name="qv_bf", align_bytes=64)
+
+        def bcols(half):
+            return slice(half * BANK, (half + 1) * BANK)
+
+        def slots(half):
+            return slice(half * HALF, (half + 1) * HALF)
+
+        def picked(window, offsets, half):
+            return window[:].indirect(offsets[:, half * LIST_COLS : (half + 1) * LIST_COLS])
+
+        def evac_v(dst, bank, half):
+            nc.vector.tensor_copy(dst[:, bcols(half)], bank[:])
+
+        def evac_s(dst, bank, half):
+            nc.scalar.copy(dst[:, bcols(half)], bank[:])
+
+        def gather_v(dst, window, offsets, half):
+            nc.vector.tensor_copy(dst, picked(window, offsets, half))
+
+        def gather_s(dst, window, offsets, half, scale=1.0):
+            nc.scalar.activation(dst, picked(window, offsets, half), COPY, scale=scale)
+
+        def piece(name):
+            return keep.tile([P, HALF], F32, name=name, tag=name)
+
+        def larger(half, d0_g):
+            nc.vector.tensor_tensor(w[:, slots(half)], a_g[:, slots(half)], d0_g[:], ALU.max)
+
+        def lower(half, b_g):
+            nc.vector.tensor_tensor(r[:, slots(half)], w[:, slots(half)], b_g[:], ALU.min)
+
+        def scatter(half, c0_neg):
+            nc.vector.tensor_tensor(picked(f1, idx3, half), r[:, slots(half)], c0_neg[:], ALU.add)
+
+        make_qv()
+        d_banks = [product("d%d" % h, st_codes, st_scales, shelves_w, shelves_sc, True, h) for h in range(2)]
+        nc.scalar.activation(qv_bf[:], qv_bank[:].rearrange("p t q -> p q t"), COPY)
+        qv_codes, qv_scales = quantise("qv", qv_bf)
+        evac_v(d0_sb, d_banks[0], 0)
+        evac_s(d0_sb, d_banks[1], 1)
+        c_banks = [product("c%d" % h, st_codes, st_scales, users_w, users_sc, False, h) for h in range(2)]
+        evac_v(c0_sb, c_banks[0], 0)
+        evac_s(c0_sb, c_banks[1], 1)
+        b_banks = [product("b%d" % h, qv_codes, qv_scales, notes_w, notes_sc, True, h) for h in range(2)]
+        evac_v(b_sb, b_banks[0], 0)
+        evac_s(b_sb, b_banks[1], 1)
+        a_banks = [product(tag, qv_codes, qv_scales, keys_w, keys_sc, False, h) for h, tag in enumerate(("a0", "shared"))]
+        d0_g = piece("d0_g")
+        gather_s(d0_g[:], d0_sb, idx4, 0)
+        c0_neg = piece("c0_neg")
+        gather_s(c0_neg[:], c0_sb, idx3, 0, scale=-1.0)
+        b_g = piece("b_g")
+        gather_v(b_g[:], b_sb, idx2, 0)
+        evac_v(a_sb, a_banks[0], 0)
+        evac_s(a_sb, a_banks[1], 1)
+        gather_v(a_g[:, slots(0)], a_sb, idx, 0)
+        gather_s(a_g[:, slots(1)], a_sb, idx, 1)
+        larger(0, d0_g)
+        lower(0, b_g)
+        scatter(0, c0_neg)
+        d0_g = piece("d0_g")
+        gather_s(d0_g[:], d0_sb, idx4, 1)
+        b_g = piece("b_g")
+        gather_s(b_g[:], b_sb, idx2, 1)
+        c0_neg = piece("c0_neg")
+        gather_s(c0_neg[:], c0_sb, idx3, 1, scale=-1.0)
+        larger(1, d0_g)
+        lower(1, b_g)
+        scatter(1, c0_neg)
+        nc.vector.tensor_tensor(cc[:], c0_sb[:], f1[:], ALU.add)
+        nc.vector.tensor_tensor(y[:, slots(0)], picked(cc, idx5, 0), w[:, slots(0)], ALU.add)
+        nc.scalar.activation(cc_g[:], picked(cc, idx5, 1), COPY)
+        nc.sync.dma_start(out[:, slots(0)], y[:, slots(0)])
+        nc.vector.tensor_tensor(y[:, slots(1)], cc_g[:], w[:, slots(1)], ALU.add)
+        nc.sync.dma_start(out[:, slots(1)], y[:, slots(1)])

@@ -58,30 +58,33 @@ def tile_attend_substitutes_madefour_kernel(
             nc.sync.dma_start(tile[:], source)
             return tile
 
-        keys_sc = zeroed_scales(nc.gpsimd, "keys_sc", COLS)
+        shelves_sc = zeroed_scales(nc.gpsimd, "shelves_sc", COLS)
         wq_sc = zeroed_scales(nc.vector, "wq_sc", K)
-        shelves_sc = zeroed_scales(nc.vector, "shelves_sc", COLS)
-        users_sc = zeroed_scales(nc.vector, "users_sc", COLS)
         notes_sc = zeroed_scales(nc.vector, "notes_sc", COLS)
+        keys_sc = zeroed_scales(nc.vector, "keys_sc", COLS)
+        users_sc = zeroed_scales(nc.vector, "users_sc", COLS)
         f1 = keep.tile([P, COLS], F32, name="f1")
         states_sb = keep.tile([P, PACK, Q], F32, name="states_sb")
         nc.vector.memset(f1[:], 0.0)
-        load_scales(nc.scalar, wq_sc, wq_scales)
         nc.sync.dma_start(states_sb[:], states.rearrange("(p t) q -> p t q", t=PACK))
+        load_scales(nc.sync, wq_sc, wq_scales)
         wq_raw = load_fp8(nc.sync, "wq_raw", wq_words)
         shelves_w = load_fp4(nc.sync, "shelves_w", shelves_words)
-        load_scales(nc.gpsimd, keys_sc, keys_scales, (0, 1))
-        users_w = load_fp8(nc.gpsimd, "users_w", users_words)
-        notes_w = load_fp4(nc.gpsimd, "notes_w", notes_words)
-        keys_w = load_fp8(nc.gpsimd, "keys_w", keys_words)
-        load_scales(nc.gpsimd, keys_sc, keys_scales, (2, 3))
-        load_scales(nc.sync, shelves_sc, shelves_scales)
-        load_scales(nc.sync, users_sc, users_scales)
+        load_scales(nc.gpsimd, shelves_sc, shelves_scales, (3,))
+        load_scales(nc.sync, shelves_sc, shelves_scales, (0, 1, 2))
+        notes_w = load_fp4(nc.sync, "notes_w", notes_words)
+        load_scales(nc.gpsimd, notes_sc, notes_scales, (3,))
+        load_scales(nc.sync, notes_sc, notes_scales, (0, 1, 2))
         idx4 = load_list("idx4", offs4)
-        load_scales(nc.sync, notes_sc, notes_scales)
-        idx3 = load_list("idx3", offs3)
+        keys_w = load_fp8(nc.sync, "keys_w", keys_words)
         idx2 = load_list("idx2", offs2)
+        load_scales(nc.gpsimd, keys_sc, keys_scales, (3,))
+        load_scales(nc.sync, keys_sc, keys_scales, (0, 1, 2))
+        users_w = load_fp8(nc.sync, "users_w", users_words)
+        load_scales(nc.gpsimd, users_sc, users_scales, (3,))
+        load_scales(nc.sync, users_sc, users_scales, (0, 1, 2))
         idx = load_list("idx", offs)
+        idx3 = load_list("idx3", offs3)
         idx5 = load_list("idx5", offs5)
 
         def quantise(name, grouped):
@@ -95,15 +98,15 @@ def tile_attend_substitutes_madefour_kernel(
         wq_sc_dealt = keep.tile([P, K], U8, name="wq_sc_dealt", align_bytes=64)
         wq_dealt = keep.tile([P, K], U32, name="wq_dealt", align_bytes=64)
         states_bf = keep.tile([P, Q, PACK], BF16, name="states_bf", align_bytes=64)
-        nc.vector.tensor_copy(
-            wq_sc_dealt[:].rearrange("p (t m) -> p m t", t=PACK), wq_sc[:].rearrange("p (m t) -> p m t", t=PACK)
-        )
         nc.vector.tensor_copy(states_bf[:], states_sb[:].rearrange("p t q -> p q t"))
+        nc.vector.tensor_copy(
+            wq_sc_dealt[:].rearrange("p (t m) -> p t m", t=PACK), wq_sc[:].rearrange("p (m t) -> p t m", t=PACK)
+        )
+        st_codes, st_scales = quantise("st", states_bf)
         nc.vector.tensor_copy(
             wq_dealt[:].bitcast(I32).rearrange("p (t m) -> p m t", t=PACK),
             wq_raw[:].bitcast(I32).rearrange("p (m t) -> p m t", t=PACK),
         )
-        st_codes, st_scales = quantise("st", states_bf)
 
         qv_bank = psum.tile([P, PACK, Q], F32, name="qv_bank", tag="shared")
         def make_qv():
@@ -156,8 +159,11 @@ def tile_attend_substitutes_madefour_kernel(
         def evac_s(dst, bank, half):
             nc.scalar.copy(dst[:, bcols(half)], bank[:])
 
-        def gather_v(dst, window, offsets, half):
-            nc.vector.tensor_copy(dst, picked(window, offsets, half))
+        def gather_v(dst, window, offsets, half, scale=None):
+            if scale is None:
+                nc.vector.tensor_copy(dst, picked(window, offsets, half))
+            else:
+                nc.vector.tensor_scalar(dst, picked(window, offsets, half), scale, 0.0, ALU.mult, ALU.add)
 
         def gather_s(dst, window, offsets, half, scale=1.0):
             nc.scalar.activation(dst, picked(window, offsets, half), COPY, scale=scale)
@@ -180,36 +186,35 @@ def tile_attend_substitutes_madefour_kernel(
         qv_codes, qv_scales = quantise("qv", qv_bf)
         evac_v(d0_sb, d_banks[0], 0)
         evac_s(d0_sb, d_banks[1], 1)
-        c_banks = [product("c%d" % h, st_codes, st_scales, users_w, users_sc, False, h) for h in range(2)]
-        evac_v(c0_sb, c_banks[0], 0)
-        evac_s(c0_sb, c_banks[1], 1)
         b_banks = [product("b%d" % h, qv_codes, qv_scales, notes_w, notes_sc, True, h) for h in range(2)]
         evac_v(b_sb, b_banks[0], 0)
         evac_s(b_sb, b_banks[1], 1)
-        a_banks = [product(tag, qv_codes, qv_scales, keys_w, keys_sc, False, h) for h, tag in enumerate(("a0", "shared"))]
-        d0_g = piece("d0_g")
-        gather_s(d0_g[:], d0_sb, idx4, 0)
-        c0_neg = piece("c0_neg")
-        gather_s(c0_neg[:], c0_sb, idx3, 0, scale=-1.0)
-        b_g = piece("b_g")
-        gather_v(b_g[:], b_sb, idx2, 0)
+        d0_g = [piece("d0_g%d" % h) for h in range(2)]
+        b_g = [piece("b_g%d" % h) for h in range(2)]
+        gather_v(d0_g[0][:], d0_sb, idx4, 0)
+        gather_s(d0_g[1][:], d0_sb, idx4, 1)
+        a_banks = [product("a%d" % h, qv_codes, qv_scales, keys_w, keys_sc, False, h) for h in range(2)]
         evac_v(a_sb, a_banks[0], 0)
         evac_s(a_sb, a_banks[1], 1)
+        gather_v(b_g[0][:], b_sb, idx2, 0)
+        gather_s(b_g[1][:], b_sb, idx2, 1)
+        c_banks = [product(tag, st_codes, st_scales, users_w, users_sc, False, h) for h, tag in enumerate(("c0", "shared"))]
+        evac_v(c0_sb, c_banks[0], 0)
+        evac_s(c0_sb, c_banks[1], 1)
         gather_v(a_g[:, slots(0)], a_sb, idx, 0)
         gather_s(a_g[:, slots(1)], a_sb, idx, 1)
-        larger(0, d0_g)
-        lower(0, b_g)
-        scatter(0, c0_neg)
-        d0_g = piece("d0_g")
-        gather_s(d0_g[:], d0_sb, idx4, 1)
-        b_g = piece("b_g")
-        gather_s(b_g[:], b_sb, idx2, 1)
-        c0_neg = piece("c0_neg")
-        gather_s(c0_neg[:], c0_sb, idx3, 1, scale=-1.0)
-        larger(1, d0_g)
-        lower(1, b_g)
-        scatter(1, c0_neg)
-        nc.vector.tensor_tensor(cc[:], c0_sb[:], f1[:], ALU.add)
+        c0_neg = [piece("c0_neg%d" % h) for h in range(2)]
+        gather_s(c0_neg[0][:], c0_sb, idx3, 0, scale=-1.0)
+        gather_s(c0_neg[1][:], c0_sb, idx3, 1, scale=-1.0)
+        larger(0, d0_g[0])
+        larger(1, d0_g[1])
+        lower(0, b_g[0])
+        lower(1, b_g[1])
+        scatter(0, c0_neg[0])
+        scatter(1, c0_neg[1])
+        nc.gpsimd.tensor_tensor(cc[:, 768:], c0_sb[:, 768:], f1[:, 768:], ALU.add)
+        nc.vector.tensor_tensor(cc[:, :BANK], c_banks[0][:], f1[:, :BANK], ALU.add)
+        nc.vector.tensor_tensor(cc[:, BANK:768], c_banks[1][:, :256], f1[:, BANK:768], ALU.add)
         nc.vector.tensor_tensor(y[:, slots(0)], picked(cc, idx5, 0), w[:, slots(0)], ALU.add)
         nc.scalar.activation(cc_g[:], picked(cc, idx5, 1), COPY)
         nc.sync.dma_start(out[:, slots(0)], y[:, slots(0)])

@@ -44,7 +44,7 @@ def tile_attend_substitutes_madefour_kernel(
                 queue.dma_start(tile[r:P:32, :].bitcast(I32), rows[r].bitcast(I32))
 
         def load_fp8(queue, name, words):
-            tile = keep.tile([P, words.shape[2]], U32, name=name, align_bytes=64)
+            tile = keep.tile([P, words.shape[2]], U32, name=name, tag=name, align_bytes=64)
             queue.dma_start(tile[:].bitcast(I32), words[0].rearrange("p n t -> p (n t)").bitcast(I32))
             return tile
 
@@ -66,24 +66,35 @@ def tile_attend_substitutes_madefour_kernel(
         f1 = keep.tile([P, COLS], F32, name="f1")
         states_sb = keep.tile([P, PACK, Q], F32, name="states_sb")
         nc.vector.memset(f1[:], 0.0)
+        load_scales(nc.gpsimd, shelves_sc, shelves_scales, (3,))
+        load_scales(nc.gpsimd, notes_sc, notes_scales, (3,))
+        load_scales(nc.gpsimd, keys_sc, keys_scales, (3,))
+        load_scales(nc.gpsimd, users_sc, users_scales, (3,))
         nc.sync.dma_start(states_sb[:], states.rearrange("(p t) q -> p t q", t=PACK))
-        load_scales(nc.sync, wq_sc, wq_scales)
+        load_scales(nc.sync, wq_sc, wq_scales, (0,))
+        load_scales(nc.sync, wq_sc, wq_scales, (1,))
+        load_scales(nc.sync, wq_sc, wq_scales, (2,))
+        load_scales(nc.sync, wq_sc, wq_scales, (3,))
         wq_raw = load_fp8(nc.sync, "wq_raw", wq_words)
         shelves_w = load_fp4(nc.sync, "shelves_w", shelves_words)
-        load_scales(nc.gpsimd, shelves_sc, shelves_scales, (3,))
-        load_scales(nc.sync, shelves_sc, shelves_scales, (0, 1, 2))
+        load_scales(nc.sync, shelves_sc, shelves_scales, (0,))
+        load_scales(nc.sync, shelves_sc, shelves_scales, (1,))
+        load_scales(nc.sync, shelves_sc, shelves_scales, (2,))
         notes_w = load_fp4(nc.sync, "notes_w", notes_words)
-        load_scales(nc.gpsimd, notes_sc, notes_scales, (3,))
-        load_scales(nc.sync, notes_sc, notes_scales, (0, 1, 2))
+        load_scales(nc.sync, notes_sc, notes_scales, (0,))
+        load_scales(nc.sync, notes_sc, notes_scales, (1,))
+        load_scales(nc.sync, notes_sc, notes_scales, (2,))
         idx4 = load_list("idx4", offs4)
         keys_w = load_fp8(nc.sync, "keys_w", keys_words)
         idx2 = load_list("idx2", offs2)
-        load_scales(nc.gpsimd, keys_sc, keys_scales, (3,))
-        load_scales(nc.sync, keys_sc, keys_scales, (0, 1, 2))
+        load_scales(nc.sync, keys_sc, keys_scales, (0,))
+        load_scales(nc.sync, keys_sc, keys_scales, (1,))
+        load_scales(nc.sync, keys_sc, keys_scales, (2,))
         users_w = load_fp8(nc.sync, "users_w", users_words)
-        load_scales(nc.gpsimd, users_sc, users_scales, (3,))
-        load_scales(nc.sync, users_sc, users_scales, (0, 1, 2))
         idx = load_list("idx", offs)
+        load_scales(nc.sync, users_sc, users_scales, (0,))
+        load_scales(nc.sync, users_sc, users_scales, (1,))
+        load_scales(nc.sync, users_sc, users_scales, (2,))
         idx3 = load_list("idx3", offs3)
         idx5 = load_list("idx5", offs5)
 
@@ -138,7 +149,6 @@ def tile_attend_substitutes_madefour_kernel(
         d0_sb = keep.tile([P, COLS], F32, name="d0_sb")
         cc = keep.tile([P, COLS], F32, name="cc")
         a_g = keep.tile([P, SLOTS], F32, name="a_g")
-        w = keep.tile([P, SLOTS], F32, name="w")
         r = keep.tile([P, SLOTS], F32, name="r")
         cc_g = keep.tile([P, HALF], F32, name="cc_g")
         y = keep.tile([P, SLOTS], F32, name="y")
@@ -180,32 +190,38 @@ def tile_attend_substitutes_madefour_kernel(
         def scatter(half, c0_neg):
             nc.vector.tensor_tensor(picked(f1, idx3, half), r[:, slots(half)], c0_neg[:], ALU.add)
 
-        make_qv()
-        d_banks = [product("d%d" % h, st_codes, st_scales, shelves_w, shelves_sc, True, h) for h in range(2)]
-        nc.scalar.activation(qv_bf[:], qv_bank[:].rearrange("p t q -> p q t"), COPY)
-        qv_codes, qv_scales = quantise("qv", qv_bf)
-        evac_v(d0_sb, d_banks[0], 0)
-        evac_s(d0_sb, d_banks[1], 1)
-        b_banks = [product("b%d" % h, qv_codes, qv_scales, notes_w, notes_sc, True, h) for h in range(2)]
-        evac_v(b_sb, b_banks[0], 0)
-        evac_s(b_sb, b_banks[1], 1)
         d0_g = [piece("d0_g%d" % h) for h in range(2)]
         b_g = [piece("b_g%d" % h) for h in range(2)]
+        c0_neg = [piece("c0_neg%d" % h) for h in range(2)]
+        banks = {}
+        make_qv()
+        banks["d0"] = product("d0", st_codes, st_scales, shelves_w, shelves_sc, True, 0)
+        banks["d1"] = product("d1", st_codes, st_scales, shelves_w, shelves_sc, True, 1)
+        nc.scalar.activation(qv_bf[:], qv_bank[:].rearrange("p t q -> p q t"), COPY)
+        qv_codes, qv_scales = quantise("qv", qv_bf)
+        evac_s(d0_sb, banks["d0"], 0)
+        evac_s(d0_sb, banks["d1"], 1)
+        banks["b0"] = product("b0", qv_codes, qv_scales, notes_w, notes_sc, True, 0)
+        banks["b1"] = product("b1", qv_codes, qv_scales, notes_w, notes_sc, True, 1)
+        evac_s(b_sb, banks["b0"], 0)
+        evac_s(b_sb, banks["b1"], 1)
         gather_v(d0_g[0][:], d0_sb, idx4, 0)
-        gather_s(d0_g[1][:], d0_sb, idx4, 1)
-        a_banks = [product("a%d" % h, qv_codes, qv_scales, keys_w, keys_sc, False, h) for h in range(2)]
-        evac_v(a_sb, a_banks[0], 0)
-        evac_s(a_sb, a_banks[1], 1)
+        gather_v(d0_g[1][:], d0_sb, idx4, 1)
+        banks["a0"] = product("a0", qv_codes, qv_scales, keys_w, keys_sc, False, 0)
+        banks["a1"] = product("a1", qv_codes, qv_scales, keys_w, keys_sc, False, 1)
+        evac_s(a_sb, banks["a0"], 0)
+        evac_s(a_sb, banks["a1"], 1)
         gather_v(b_g[0][:], b_sb, idx2, 0)
-        gather_s(b_g[1][:], b_sb, idx2, 1)
-        c_banks = [product(tag, st_codes, st_scales, users_w, users_sc, False, h) for h, tag in enumerate(("c0", "shared"))]
-        evac_v(c0_sb, c_banks[0], 0)
-        evac_s(c0_sb, c_banks[1], 1)
+        gather_v(b_g[1][:], b_sb, idx2, 1)
         gather_v(a_g[:, slots(0)], a_sb, idx, 0)
         gather_s(a_g[:, slots(1)], a_sb, idx, 1)
-        c0_neg = [piece("c0_neg%d" % h) for h in range(2)]
+        banks["c0"] = product("c0", st_codes, st_scales, users_w, users_sc, False, 0)
+        banks["c1"] = product("shared", st_codes, st_scales, users_w, users_sc, False, 1)
+        evac_v(c0_sb, banks["c0"], 0)
+        evac_s(c0_sb, banks["c1"], 1)
         gather_s(c0_neg[0][:], c0_sb, idx3, 0, scale=-1.0)
         gather_s(c0_neg[1][:], c0_sb, idx3, 1, scale=-1.0)
+        w = keep.tile([P, SLOTS], F32, name="w", tag="users_w", align_bytes=64)
         larger(0, d0_g[0])
         larger(1, d0_g[1])
         lower(0, b_g[0])
@@ -213,8 +229,8 @@ def tile_attend_substitutes_madefour_kernel(
         scatter(0, c0_neg[0])
         scatter(1, c0_neg[1])
         nc.gpsimd.tensor_tensor(cc[:, 768:], c0_sb[:, 768:], f1[:, 768:], ALU.add)
-        nc.vector.tensor_tensor(cc[:, :BANK], c_banks[0][:], f1[:, :BANK], ALU.add)
-        nc.vector.tensor_tensor(cc[:, BANK:768], c_banks[1][:, :256], f1[:, BANK:768], ALU.add)
+        nc.vector.tensor_tensor(cc[:, :BANK], banks["c0"][:], f1[:, :BANK], ALU.add)
+        nc.vector.tensor_tensor(cc[:, BANK:768], banks["c1"][:, :256], f1[:, BANK:768], ALU.add)
         nc.vector.tensor_tensor(y[:, slots(0)], picked(cc, idx5, 0), w[:, slots(0)], ALU.add)
         nc.scalar.activation(cc_g[:], picked(cc, idx5, 1), COPY)
         nc.sync.dma_start(out[:, slots(0)], y[:, slots(0)])

from contextlib import ExitStack

import concourse.mybir as mybir

D, K, COLS, SLOTS, Q = 512, 512, 1024, 512, 128
FLOPS = 2 * D * K * Q + 4 * 2 * K * COLS * Q

F32 = mybir.dt.float32
BF16 = mybir.dt.bfloat16
I32 = mybir.dt.int32
U32 = mybir.dt.uint32
U16 = mybir.dt.uint16
U8 = mybir.dt.uint8
FP8X4 = mybir.dt.float8_e4m3fn_x4
FP4X4 = mybir.dt.float4_e2m1fn_x4
ALU = mybir.AluOpType
COPY = mybir.ActivationFunctionType.Copy

P = 128
PACK = 4
BANK = 512
HALF = SLOTS // 2
LIST_COLS = HALF // 16


def tile_attend_substitutes_madefour_kernel(
    tc, states, wq_words, wq_scales, keys_words, keys_scales, notes_words, notes_scales,
    users_words, users_scales, shelves_words, shelves_scales, offs, offs2, offs3, offs4, offs5, out,
):
    nc = tc.nc
    with ExitStack() as ctx:
        lists = ctx.enter_context(tc.tile_pool(name="lists", bufs=1))
        keep = ctx.enter_context(tc.tile_pool(name="keep", bufs=1))
        psum = ctx.enter_context(tc.psum_pool(name="psum", bufs=1))

        def zeroed_scales(engine, name, width):
            tile = keep.tile([P, width], U8, name=name, align_bytes=64)
            engine.memset(tile[:].bitcast(I32), 0)
            return tile

        def load_scales(queue, tile, scales, which=range(4)):
            rows = scales[0].rearrange("(quad r) n -> r quad n", r=4)
            for r in which:
                queue.dma_start(tile[r:P:32, :].bitcast(I32), rows[r].bitcast(I32))

        def load_fp8(queue, name, words):
            tile = keep.tile([P, words.shape[2]], U32, name=name, tag=name, align_bytes=64)
            queue.dma_start(tile[:].bitcast(I32), words[0].rearrange("p n t -> p (n t)").bitcast(I32))
            return tile

        def load_fp4(queue, name, words):
            tile = keep.tile([P, words.shape[2]], U8, name=name, align_bytes=64)
            queue.dma_start(tile[:].bitcast(I32), words[0].bitcast(I32))
            return tile

        def load_list(name, source):
            tile = lists.tile([P, SLOTS // 16], U16, name=name)
            nc.sync.dma_start(tile[:], source)
            return tile

        shelves_sc = zeroed_scales(nc.gpsimd, "shelves_sc", COLS)
        wq_sc = zeroed_scales(nc.vector, "wq_sc", K)
        notes_sc = zeroed_scales(nc.vector, "notes_sc", COLS)
        keys_sc = zeroed_scales(nc.vector, "keys_sc", COLS)
        users_sc = zeroed_scales(nc.vector, "users_sc", COLS)
        f1 = keep.tile([P, COLS], F32, name="f1")
        states_sb = keep.tile([P, PACK, Q], F32, name="states_sb")
        nc.vector.memset(f1[:], 0.0)
        load_scales(nc.gpsimd, shelves_sc, shelves_scales, (3,))
        load_scales(nc.gpsimd, notes_sc, notes_scales, (3,))
        load_scales(nc.gpsimd, keys_sc, keys_scales, (3,))
        load_scales(nc.gpsimd, users_sc, users_scales, (3,))
        nc.sync.dma_start(states_sb[:], states.rearrange("(p t) q -> p t q", t=PACK))
        load_scales(nc.sync, wq_sc, wq_scales, (0,))
        load_scales(nc.sync, wq_sc, wq_scales, (1,))
        load_scales(nc.sync, wq_sc, wq_scales, (2,))
        load_scales(nc.sync, wq_sc, wq_scales, (3,))
        wq_raw = load_fp8(nc.sync, "wq_raw", wq_words)
        shelves_w = load_fp4(nc.sync, "shelves_w", shelves_words)
        load_scales(nc.sync, shelves_sc, shelves_scales, (0,))
        load_scales(nc.sync, shelves_sc, shelves_scales, (1,))
        load_scales(nc.sync, shelves_sc, shelves_scales, (2,))
        notes_w = load_fp4(nc.sync, "notes_w", notes_words)
        load_scales(nc.sync, notes_sc, notes_scales, (0,))
        load_scales(nc.sync, notes_sc, notes_scales, (1,))
        load_scales(nc.sync, notes_sc, notes_scales, (2,))
        idx4 = load_list("idx4", offs4)
        keys_w = load_fp8(nc.sync, "keys_w", keys_words)
        idx2 = load_list("idx2", offs2)
        load_scales(nc.sync, keys_sc, keys_scales, (0,))
        load_scales(nc.sync, keys_sc, keys_scales, (1,))
        load_scales(nc.sync, keys_sc, keys_scales, (2,))
        users_w = load_fp8(nc.sync, "users_w", users_words)
        idx = load_list("idx", offs)
        load_scales(nc.sync, users_sc, users_scales, (0,))
        load_scales(nc.sync, users_sc, users_scales, (1,))
        load_scales(nc.sync, users_sc, users_scales, (2,))
        idx3 = load_list("idx3", offs3)
        idx5 = load_list("idx5", offs5)

        def quantise(name, grouped):
            codes = keep.tile([P, Q], U32, name=name + "_codes", align_bytes=64)
            scales = keep.tile([P, Q], U8, name=name + "_scales", align_bytes=64)
            nc.vector.quantize_mx(
                out=codes[:].bitcast(FP8X4), scales=scales[:], in_=grouped[:].rearrange("p q t -> p (q t)")
            )
            return codes, scales

        wq_sc_dealt = keep.tile([P, K], U8, name="wq_sc_dealt", align_bytes=64)
        wq_dealt = keep.tile([P, K], U32, name="wq_dealt", align_bytes=64)
        states_bf = keep.tile([P, Q, PACK], BF16, name="states_bf", align_bytes=64)
        nc.vector.tensor_copy(states_bf[:], states_sb[:].rearrange("p t q -> p q t"))
        nc.vector.tensor_copy(
            wq_sc_dealt[:].rearrange("p (t m) -> p t m", t=PACK), wq_sc[:].rearrange("p (m t) -> p t m", t=PACK)
        )
        st_codes, st_scales = quantise("st", states_bf)
        nc.vector.tensor_copy(
            wq_dealt[:].bitcast(I32).rearrange("p (t m) -> p m t", t=PACK),
            wq_raw[:].bitcast(I32).rearrange("p (m t) -> p m t", t=PACK),
        )

        qv_bank = psum.tile([P, PACK, Q], F32, name="qv_bank", tag="shared")
        def make_qv():
            for t in range(PACK):
                cols = slice(t * P, (t + 1) * P)
                nc.tensor.matmul_mx(
                    out=qv_bank[:, t, :],
                    lhsT=wq_dealt[:, cols].bitcast(FP8X4), lhsT_scale=wq_sc_dealt[:, cols],
                    rhs=st_codes[:].bitcast(FP8X4), rhs_scale=st_scales[:],
                    start=True, stop=True,
                )

        def product(tag, codes, scales, words, word_scales, fp4, half):
            bank = psum.tile([P, BANK], F32, name="bank_" + tag, tag=tag)
            cols = slice(half * BANK, (half + 1) * BANK)
            if fp4:
                moving = words[:, 2 * cols.start : 2 * cols.stop].bitcast(FP4X4)
            else:
                moving = words[:, cols].bitcast(FP8X4)
            nc.tensor.matmul_mx(
                out=bank[:], lhsT=codes[:].bitcast(FP8X4), lhsT_scale=scales[:],
                rhs=moving, rhs_scale=word_scales[:, cols], start=True, stop=True,
            )
            return bank

        a_sb = keep.tile([P, COLS], F32, name="a_sb")
        b_sb = keep.tile([P, COLS], F32, name="b_sb")
        c0_sb = keep.tile([P, COLS], F32, name="c0_sb")
        d0_sb = keep.tile([P, COLS], F32, name="d0_sb")
        cc = keep.tile([P, COLS], F32, name="cc")
        a_g = keep.tile([P, SLOTS], F32, name="a_g")
        r = keep.tile([P, SLOTS], F32, name="r")
        cc_g = keep.tile([P, HALF], F32, name="cc_g")
        y = keep.tile([P, SLOTS], F32, name="y")
        qv_bf = keep.tile([P, Q, PACK], BF16, name="qv_bf", align_bytes=64)

        def bcols(half):
            return slice(half * BANK, (half + 1) * BANK)

        def slots(half):
            return slice(half * HALF, (half + 1) * HALF)

        def picked(window, offsets, half):
            return window[:].indirect(offsets[:, half * LIST_COLS : (half + 1) * LIST_COLS])

        def evac_v(dst, bank, half):
            nc.vector.tensor_copy(dst[:, bcols(half)], bank[:])

        def evac_s(dst, bank, half):
            nc.scalar.copy(dst[:, bcols(half)], bank[:])

        def gather_v(dst, window, offsets, half, scale=None):
            if scale is None:
                nc.vector.tensor_copy(dst, picked(window, offsets, half))
            else:
                nc.vector.tensor_scalar(dst, picked(window, offsets, half), scale, 0.0, ALU.mult, ALU.add)

        def gather_s(dst, window, offsets, half, scale=1.0):
            nc.scalar.activation(dst, picked(window, offsets, half), COPY, scale=scale)

        def piece(name):
            return keep.tile([P, HALF], F32, name=name, tag=name)

        def larger(half, d0_g):
            nc.vector.tensor_tensor(w[:, slots(half)], a_g[:, slots(half)], d0_g[:], ALU.max)

        def lower(half, b_g):
            nc.vector.tensor_tensor(r[:, slots(half)], w[:, slots(half)], b_g[:], ALU.min)

        def scatter(half, c0_neg):
            nc.vector.tensor_tensor(picked(f1, idx3, half), r[:, slots(half)], c0_neg[:], ALU.add)

        d0_g = [piece("d0_g%d" % h) for h in range(2)]
        b_g = [piece("b_g%d" % h) for h in range(2)]
        c0_neg = [piece("c0_neg%d" % h) for h in range(2)]
        banks = {}
        make_qv()
        banks["d0"] = product("d0", st_codes, st_scales, shelves_w, shelves_sc, True, 0)
        banks["d1"] = product("d1", st_codes, st_scales, shelves_w, shelves_sc, True, 1)
        nc.scalar.activation(qv_bf[:], qv_bank[:].rearrange("p t q -> p q t"), COPY)
        qv_codes, qv_scales = quantise("qv", qv_bf)
        evac_s(d0_sb, banks["d0"], 0)
        evac_s(d0_sb, banks["d1"], 1)
        banks["b0"] = product("b0", qv_codes, qv_scales, notes_w, notes_sc, True, 0)
        banks["b1"] = product("b1", qv_codes, qv_scales, notes_w, notes_sc, True, 1)
        evac_s(b_sb, banks["b0"], 0)
        evac_s(b_sb, banks["b1"], 1)
        gather_v(d0_g[0][:], d0_sb, idx4, 0)
        gather_v(d0_g[1][:], d0_sb, idx4, 1)
        banks["a0"] = product("a0", qv_codes, qv_scales, keys_w, keys_sc, False, 0)
        banks["a1"] = product("a1", qv_codes, qv_scales, keys_w, keys_sc, False, 1)
        evac_s(a_sb, banks["a0"], 0)
        evac_s(a_sb, banks["a1"], 1)
        gather_v(b_g[0][:], b_sb, idx2, 0)
        gather_v(b_g[1][:], b_sb, idx2, 1)
        gather_v(a_g[:, slots(0)], a_sb, idx, 0)
        gather_s(a_g[:, slots(1)], a_sb, idx, 1)
        banks["c0"] = product("c0", st_codes, st_scales, users_w, users_sc, False, 0)
        banks["c1"] = product("shared", st_codes, st_scales, users_w, users_sc, False, 1)
        evac_v(c0_sb, banks["c0"], 0)
        evac_s(c0_sb, banks["c1"], 1)
        gather_s(c0_neg[0][:], c0_sb, idx3, 0, scale=-1.0)
        gather_s(c0_neg[1][:], c0_sb, idx3, 1, scale=-1.0)
        w = keep.tile([P, SLOTS], F32, name="w", tag="users_w", align_bytes=64)
        larger(0, d0_g[0])
        larger(1, d0_g[1])
        lower(0, b_g[0])
        lower(1, b_g[1])
        scatter(0, c0_neg[0])
        scatter(1, c0_neg[1])
        nc.gpsimd.tensor_tensor(cc[:, 768:], c0_sb[:, 768:], f1[:, 768:], ALU.add)
        nc.vector.tensor_tensor(cc[:, :BANK], banks["c0"][:], f1[:, :BANK], ALU.add)
        nc.vector.tensor_tensor(cc[:, BANK:768], banks["c1"][:, :256], f1[:, BANK:768], ALU.add)
        nc.vector.tensor_tensor(y[:, slots(0)], picked(cc, idx5, 0), w[:, slots(0)], ALU.add)
        nc.scalar.activation(cc_g[:], picked(cc, idx5, 1), COPY)
        nc.sync.dma_start(out[:, slots(0)], y[:, slots(0)])
        nc.vector.tensor_tensor(y[:, slots(1)], cc_g[:], w[:, slots(1)], ALU.add)
        nc.sync.dma_start(out[:, slots(1)], y[:, slots(1)])
